import numpy as np
import ml_dtypes


def mxq(x, axis, fmt="e4m3"):
    dtype, down = {"e4m3": (ml_dtypes.float8_e4m3fn, 7), "e5m2": (ml_dtypes.float8_e5m2, 14)}[fmt]
    v = np.moveaxis(np.asarray(x, np.float32).astype(ml_dtypes.bfloat16).astype(np.float64), axis, -1)
    blocks = v.reshape(v.shape[:-1] + (-1, 32))
    amax = np.abs(blocks).max(-1, keepdims=True)
    byte = np.maximum(np.where(amax > 0, np.frexp(amax)[1] - 1 + 127, 0) - down, 1)
    scale = np.exp2(byte - 127.0)
    codes = (blocks / scale).astype(np.float32).astype(dtype).astype(np.float64)
    return np.moveaxis((codes * scale).reshape(v.shape), -1, axis)


WIDE = False


def mx_kscale(k):
    if not WIDE:
        return np.ones(k)
    levels = np.array([10, -10, 5, -5, 0])
    if k % 512:
        return np.exp2(np.random.permutation(np.resize(levels, k // 32))).repeat(32)
    a = np.empty((k // 512, 16))
    for p in range(k // 512):
        a[p, :8] = np.random.permutation(np.resize(levels, 8))
        for g in range(8):
            far = levels[np.abs(levels - a[p, g]) >= 10]
            a[p, g + 8] = far[np.random.randint(len(far))]
    return np.exp2(a.ravel()).repeat(32)


def f64(x):
    return np.asarray(x).astype(np.float64)


def striped(idx):
    return np.tile(idx.reshape(-1, 16).T, (8, 1)).astype(np.uint16)


def unstriped(offs):
    return offs[:16].T.reshape(-1).astype(np.int64)


def relu(v):
    return np.maximum(v, 0.0)


K, T, D, S, V, N = 512, 2048, 2, 768, 384, 256


def setup_inputs():
    n = np.random.standard_normal
    s = mx_kscale(K)[:, None]
    return {
        "xT": (n((K, T)) * s).astype(np.float32),
        "w": (n((K, N)) / np.sqrt(K) / s).astype(np.float32),
        "b": (0.3 * n((N, 1))).astype(np.float32),
        "gate": np.tile(np.random.uniform(0.2, 1.0, (D, 1, V)) / np.sqrt(D), (1, N, 1)).astype(np.float32),
        "offs": striped(np.random.permutation(T)[:S]),
        "pos1": striped(np.random.permutation(S)[:V]),
        "pos2": striped(np.random.permutation(S)[:V]),
    }


def reference(xT, w, b, gate, offs, pos1, pos2):
    idx = unstriped(offs)
    xq = mxq(f64(xT)[:, idx], 0, "e4m3")
    y = mxq(f64(w), 0, "e4m3").T @ xq
    y = relu(y + f64(b))
    return sum(f64(gate[d]) * y[:, unstriped(p)] for d, p in enumerate((pos1, pos2)))

@@ -1,0 +1,120 @@
+from contextlib import ExitStack
+
+import concourse.mybir as mybir
+
+K, T, D, S, V, N = 512, 2048, 2, 768, 384, 256
+FLOPS = 2 * K * S * N
+
+P = 128
+PACK = 4
+BLOCKS = N // P
+SLICE = 256
+
+F32 = mybir.dt.float32
+BF16 = mybir.dt.bfloat16
+U32 = mybir.dt.uint32
+U16 = mybir.dt.uint16
+U8 = mybir.dt.uint8
+FP8X4 = mybir.dt.float8_e4m3fn_x4
+ADD, MAX, MULT = mybir.AluOpType.add, mybir.AluOpType.max, mybir.AluOpType.mult
+RELU = mybir.ActivationFunctionType.Relu
+
+
+def tile_picked_sub_lin_relu_sub_e_kernel(tc, xT, w, b, gate, offs, pos1, pos2, out):
+    nc = tc.nc
+    with ExitStack() as ctx:
+        keep = ctx.enter_context(tc.tile_pool(name="keep", bufs=1))
+        psum = ctx.enter_context(tc.psum_pool(name="psum", bufs=1))
+
+        nodes = keep.tile([P, S // 16], U16, name="nodes")
+        nc.sync.dma_start(nodes[:], offs)
+        x_rows = xT.rearrange("(p j) t -> p j t", j=PACK)
+        planes = []
+        for j in range(PACK):
+            plane = keep.tile([P, T], F32, name=f"plane{j}", align_bytes=64)
+            nc.sync.dma_start(plane[:], x_rows[:, j, :])
+            planes.append(plane)
+        w_raw = keep.tile([P, PACK, N], F32, name="w_raw", align_bytes=64)
+        nc.sync.dma_start(w_raw[:], w.rearrange("(p j) n -> p j n", j=PACK))
+        bias = keep.tile([P, BLOCKS], F32, name="bias")
+        nc.sync.dma_start(bias[:], b.rearrange("(p c) o -> p (c o)", c=BLOCKS))
+        turns = []
+        for d, lst in enumerate((pos1, pos2)):
+            turn = keep.tile([P, V // 16], U16, name=f"turn{d}")
+            nc.sync.dma_start(turn[:], lst)
+            turns.append(turn)
+        gates = keep.tile([P, D, BLOCKS * V], F32, name="gates", align_bytes=64)
+        for d in range(D):
+            nc.sync.dma_start(gates[:, d, :], gate[d].rearrange("(p c) v -> p (c v)", c=BLOCKS))
+
+        got = keep.tile([P, PACK, S], F32, name="got", align_bytes=64)
+        grouped = keep.tile([P, S, PACK], BF16, name="grouped", align_bytes=64)
+        x_codes = keep.tile([P, S], U32, name="x_codes", align_bytes=64)
+        x_scales = keep.tile([P, S], U8, name="x_scales", align_bytes=64)
+        w_grouped = keep.tile([P, BLOCKS, P, PACK], BF16, name="w_grouped", align_bytes=64)
+        w_codes = keep.tile([P, N], U32, name="w_codes", align_bytes=64)
+        w_scales = keep.tile([P, N], U8, name="w_scales", align_bytes=64)
+
+        for j in (0, 1):
+            nc.vector.tensor_copy(got[:, j, :], planes[j][:].indirect(nodes[:]))
+        nc.scalar.copy(grouped[:, :, 0:2], got[:, 0:2, :].rearrange("p j s -> p s j"))
+        nc.vector.tensor_copy(got[:, 2, 0:512], planes[2][:].indirect(nodes[:, 0:32]))
+        nc.vector.tensor_copy(grouped[:, 512:768, 2], planes[2][:].indirect(nodes[:, 32:48]))
+        for s in (0, 1):
+            cols = slice(s * SLICE, (s + 1) * SLICE)
+            nc.vector.tensor_copy(got[:, 3, cols], planes[3][:].indirect(nodes[:, 16 * s : 16 * s + 16]))
+            nc.scalar.copy(grouped[:, cols, 2:4], got[:, 2:4, cols].rearrange("p j s -> p s j"))
+        nc.vector.tensor_copy(grouped[:, 512:768, 3], planes[3][:].indirect(nodes[:, 32:48]))
+        nc.gpsimd.tensor_scalar(
+            w_grouped[:], w_raw[:].rearrange("p j (m c) -> p c m j", c=BLOCKS), 1.0, 0.0, MULT, ADD
+        )
+
+        def quantize(codes, scales, values):
+            nc.vector.quantize_mx(out=codes.bitcast(FP8X4), scales=scales, in_=values)
+
+        y = []
+        for c in range(BLOCKS):
+            y.append(keep.tile([P, S], F32, name=f"y{c}", align_bytes=64))
+        acc = {}
+        for s in range(3):
+            cols = slice(s * SLICE, (s + 1) * SLICE)
+            quantize(x_codes[:, cols], x_scales[:, cols], grouped[:, cols, :].rearrange("p s j -> p (s j)"))
+            if s == 0:
+                quantize(w_codes[:], w_scales[:], w_grouped[:].rearrange("p c m j -> p (c m j)"))
+        for c in range(BLOCKS):
+            for s in range(3):
+                cols = slice(s * SLICE, (s + 1) * SLICE)
+                acc = psum.tile([P, SLICE], F32, name=f"acc{c}{s}")
+                nc.tensor.matmul_mx(
+                    out=acc[:],
+                    lhsT=w_codes[:, c * P : (c + 1) * P].bitcast(FP8X4),
+                    lhsT_scale=w_scales[:, c * P : (c + 1) * P],
+                    rhs=x_codes[:, cols].bitcast(FP8X4),
+                    rhs_scale=x_scales[:, cols],
+                    start=True,
+                    stop=True,
+                )
+                if c == 0 and s == 2:
+                    nc.vector.tensor_scalar(y[c][:, cols], acc[:], bias[:, c : c + 1], 0.0, ADD, MAX)
+                else:
+                    nc.scalar.activation(y[c][:, cols], acc[:], RELU, bias=bias[:, c : c + 1])
+
+        prods = {}
+
+        def fetch(c, d):
+            prods[c, d] = keep.tile([P, V], F32, name=f"prod{c}{d}", align_bytes=64)
+            nc.vector.tensor_tensor(
+                prods[c, d][:], y[c][:].indirect(turns[d][:]), gates[:, d, c * V : (c + 1) * V], MULT
+            )
+
+        def finish(c):
+            total = keep.tile([P, V], F32, name=f"total{c}", align_bytes=64)
+            nc.vector.tensor_tensor(total[:], prods[c, 0][:], prods[c, 1][:], ADD)
+            nc.sync.dma_start(out.rearrange("(p c) v -> p c v", c=BLOCKS)[:, c, :], total[:])
+
+        fetch(0, 0)
+        fetch(0, 1)
+        fetch(1, 0)
+        finish(0)
+        fetch(1, 1)
+        finish(1)

@@ -26,15 +26,18 @@ def tile_picked_sub_lin_relu_sub_e_kernel(tc, xT, w, b, gate, offs, pos1, pos2, 
         keep = ctx.enter_context(tc.tile_pool(name="keep", bufs=1))
         psum = ctx.enter_context(tc.psum_pool(name="psum", bufs=1))
 
+        def tile(shape, dtype, name):
+            return keep.tile(shape, dtype, name=name, align_bytes=64)
+
         nodes = keep.tile([P, S // 16], U16, name="nodes")
         nc.sync.dma_start(nodes[:], offs)
         x_rows = xT.rearrange("(p j) t -> p j t", j=PACK)
         planes = []
         for j in range(PACK):
-            plane = keep.tile([P, T], F32, name=f"plane{j}", align_bytes=64)
+            plane = tile([P, T], F32, f"plane{j}")
             nc.sync.dma_start(plane[:], x_rows[:, j, :])
             planes.append(plane)
-        w_raw = keep.tile([P, PACK, N], F32, name="w_raw", align_bytes=64)
+        w_raw = tile([P, PACK, N], F32, "w_raw")
         nc.sync.dma_start(w_raw[:], w.rearrange("(p j) n -> p j n", j=PACK))
         bias = keep.tile([P, BLOCKS], F32, name="bias")
         nc.sync.dma_start(bias[:], b.rearrange("(p c) o -> p (c o)", c=BLOCKS))
@@ -43,78 +46,99 @@ def tile_picked_sub_lin_relu_sub_e_kernel(tc, xT, w, b, gate, offs, pos1, pos2, 
             turn = keep.tile([P, V // 16], U16, name=f"turn{d}")
             nc.sync.dma_start(turn[:], lst)
             turns.append(turn)
-        gates = keep.tile([P, D, BLOCKS * V], F32, name="gates", align_bytes=64)
+        gates = tile([P, D, BLOCKS * V], F32, "gates")
         for d in range(D):
             nc.sync.dma_start(gates[:, d, :], gate[d].rearrange("(p c) v -> p (c v)", c=BLOCKS))
 
-        got = keep.tile([P, PACK, S], F32, name="got", align_bytes=64)
-        grouped = keep.tile([P, S, PACK], BF16, name="grouped", align_bytes=64)
-        x_codes = keep.tile([P, S], U32, name="x_codes", align_bytes=64)
-        x_scales = keep.tile([P, S], U8, name="x_scales", align_bytes=64)
-        w_grouped = keep.tile([P, BLOCKS, P, PACK], BF16, name="w_grouped", align_bytes=64)
-        w_codes = keep.tile([P, N], U32, name="w_codes", align_bytes=64)
-        w_scales = keep.tile([P, N], U8, name="w_scales", align_bytes=64)
+        got01 = tile([P, 2, S], F32, "got01")
+        got23 = tile([P, 2, SLICE], F32, "got23")
+        grouped = tile([P, S, PACK], BF16, "grouped")
+        x_codes = tile([P, S], U32, "x_codes")
+        x_scales = tile([P, S], U8, "x_scales")
+        w_grouped = [tile([P, P, PACK], BF16, f"w_grouped{c}") for c in range(BLOCKS)]
+        w_codes = [tile([P, P], U32, f"w_codes{c}") for c in range(BLOCKS)]
+        w_scales = [tile([P, P], U8, f"w_scales{c}") for c in range(BLOCKS)]
+        y = [tile([P, S], F32, f"y{c}") for c in range(BLOCKS)]
+        w_by_block = w_raw[:].rearrange("p j (m c) -> p c m j", c=BLOCKS)
 
-        for j in (0, 1):
-            nc.vector.tensor_copy(got[:, j, :], planes[j][:].indirect(nodes[:]))
-        nc.scalar.copy(grouped[:, :, 0:2], got[:, 0:2, :].rearrange("p j s -> p s j"))
-        nc.vector.tensor_copy(got[:, 2, 0:512], planes[2][:].indirect(nodes[:, 0:32]))
-        nc.vector.tensor_copy(grouped[:, 512:768, 2], planes[2][:].indirect(nodes[:, 32:48]))
-        for s in (0, 1):
-            cols = slice(s * SLICE, (s + 1) * SLICE)
-            nc.vector.tensor_copy(got[:, 3, cols], planes[3][:].indirect(nodes[:, 16 * s : 16 * s + 16]))
-            nc.scalar.copy(grouped[:, cols, 2:4], got[:, 2:4, cols].rearrange("p j s -> p s j"))
-        nc.vector.tensor_copy(grouped[:, 512:768, 3], planes[3][:].indirect(nodes[:, 32:48]))
-        nc.gpsimd.tensor_scalar(
-            w_grouped[:], w_raw[:].rearrange("p j (m c) -> p c m j", c=BLOCKS), 1.0, 0.0, MULT, ADD
-        )
+        def cut(s):
+            return slice(s * SLICE, (s + 1) * SLICE)
+
+        def fetch_a(j):
+            nc.vector.tensor_copy(got23[:, j - 2, :], planes[j][:].indirect(nodes[:, 0 : SLICE // 16]))
+
+        def fetch_b(j):
+            nc.vector.tensor_copy(grouped[:, SLICE:S, j], planes[j][:].indirect(nodes[:, SLICE // 16 : S // 16]))
+
+        def pair01():
+            nc.scalar.copy(grouped[:, :, 0:2], got01[:].rearrange("p j s -> p s j"))
+
+        def pair23():
+            nc.scalar.copy(grouped[:, cut(0), 2:4], got23[:].rearrange("p j s -> p s j"))
 
         def quantize(codes, scales, values):
             nc.vector.quantize_mx(out=codes.bitcast(FP8X4), scales=scales, in_=values)
 
-        y = []
-        for c in range(BLOCKS):
-            y.append(keep.tile([P, S], F32, name=f"y{c}", align_bytes=64))
-        acc = {}
-        for s in range(3):
-            cols = slice(s * SLICE, (s + 1) * SLICE)
-            quantize(x_codes[:, cols], x_scales[:, cols], grouped[:, cols, :].rearrange("p s j -> p (s j)"))
-            if s == 0:
-                quantize(w_codes[:], w_scales[:], w_grouped[:].rearrange("p c m j -> p (c m j)"))
-        for c in range(BLOCKS):
-            for s in range(3):
-                cols = slice(s * SLICE, (s + 1) * SLICE)
-                acc = psum.tile([P, SLICE], F32, name=f"acc{c}{s}")
-                nc.tensor.matmul_mx(
-                    out=acc[:],
-                    lhsT=w_codes[:, c * P : (c + 1) * P].bitcast(FP8X4),
-                    lhsT_scale=w_scales[:, c * P : (c + 1) * P],
-                    rhs=x_codes[:, cols].bitcast(FP8X4),
-                    rhs_scale=x_scales[:, cols],
-                    start=True,
-                    stop=True,
-                )
-                if c == 0 and s == 2:
-                    nc.vector.tensor_scalar(y[c][:, cols], acc[:], bias[:, c : c + 1], 0.0, ADD, MAX)
-                else:
-                    nc.scalar.activation(y[c][:, cols], acc[:], RELU, bias=bias[:, c : c + 1])
+        def quantize_x(s):
+            quantize(x_codes[:, cut(s)], x_scales[:, cut(s)], grouped[:, cut(s), :].rearrange("p s j -> p (s j)"))
+
+        def quantize_w(c):
+            quantize(w_codes[c][:], w_scales[c][:], w_grouped[c][:].rearrange("p m j -> p (m j)"))
+
+        def multiply(c, s, on_vector=False):
+            acc = psum.tile([P, SLICE], F32, name=f"acc{c}{s}")
+            nc.tensor.matmul_mx(
+                out=acc[:],
+                lhsT=w_codes[c][:].bitcast(FP8X4),
+                lhsT_scale=w_scales[c][:],
+                rhs=x_codes[:, cut(s)].bitcast(FP8X4),
+                rhs_scale=x_scales[:, cut(s)],
+                start=True,
+                stop=True,
+            )
+            if on_vector:
+                nc.vector.tensor_scalar(y[c][:, cut(s)], acc[:], bias[:, c : c + 1], 0.0, ADD, MAX)
+            else:
+                nc.scalar.activation(y[c][:, cut(s)], acc[:], RELU, bias=bias[:, c : c + 1])
 
         prods = {}
 
         def fetch(c, d):
-            prods[c, d] = keep.tile([P, V], F32, name=f"prod{c}{d}", align_bytes=64)
+            prods[c, d] = tile([P, V], F32, f"prod{c}{d}")
             nc.vector.tensor_tensor(
                 prods[c, d][:], y[c][:].indirect(turns[d][:]), gates[:, d, c * V : (c + 1) * V], MULT
             )
 
         def finish(c):
-            total = keep.tile([P, V], F32, name=f"total{c}", align_bytes=64)
+            total = tile([P, V], F32, f"total{c}")
             nc.vector.tensor_tensor(total[:], prods[c, 0][:], prods[c, 1][:], ADD)
             nc.sync.dma_start(out.rearrange("(p c) v -> p c v", c=BLOCKS)[:, c, :], total[:])
+
+        for j in (0, 1):
+            nc.vector.tensor_copy(got01[:, j, :], planes[j][:].indirect(nodes[:]))
+        pair01()
+        fetch_a(2)
+        fetch_b(2)
+        fetch_a(3)
+        pair23()
+        nc.scalar.copy(w_grouped[0][:], w_by_block[:, 0])
+        fetch_b(3)
+        quantize_x(0)
+        quantize_w(0)
+        multiply(0, 0)
+        quantize_x(1)
+        multiply(0, 1)
+        quantize_x(2)
+        multiply(0, 2)
+        nc.scalar.copy(w_grouped[1][:], w_by_block[:, 1])
+        quantize_w(1)
+        multiply(1, 0)
+        multiply(1, 1)
+        multiply(1, 2)
 
         fetch(0, 0)
         fetch(0, 1)
         fetch(1, 0)
-        finish(0)
         fetch(1, 1)
+        finish(0)
         finish(1)

from contextlib import ExitStack

import concourse.mybir as mybir

K, T, D, S, V, N = 512, 2048, 2, 768, 384, 256
FLOPS = 2 * K * S * N

P = 128
PACK = 4
BLOCKS = N // P
SLICE = 256

F32 = mybir.dt.float32
BF16 = mybir.dt.bfloat16
U32 = mybir.dt.uint32
U16 = mybir.dt.uint16
U8 = mybir.dt.uint8
FP8X4 = mybir.dt.float8_e4m3fn_x4
ADD, MAX, MULT = mybir.AluOpType.add, mybir.AluOpType.max, mybir.AluOpType.mult
RELU = mybir.ActivationFunctionType.Relu


def tile_picked_sub_lin_relu_sub_e_kernel(tc, xT, w, b, gate, offs, pos1, pos2, out):
    nc = tc.nc
    with ExitStack() as ctx:
        keep = ctx.enter_context(tc.tile_pool(name="keep", bufs=1))
        psum = ctx.enter_context(tc.psum_pool(name="psum", bufs=1))

        def tile(shape, dtype, name):
            return keep.tile(shape, dtype, name=name, align_bytes=64)

        nodes = keep.tile([P, S // 16], U16, name="nodes")
        nc.sync.dma_start(nodes[:], offs)
        x_rows = xT.rearrange("(p j) t -> p j t", j=PACK)
        planes = []
        for j in range(PACK):
            plane = tile([P, T], F32, f"plane{j}")
            nc.sync.dma_start(plane[:], x_rows[:, j, :])
            planes.append(plane)
        w_raw = tile([P, PACK, N], F32, "w_raw")
        nc.sync.dma_start(w_raw[:], w.rearrange("(p j) n -> p j n", j=PACK))
        bias = keep.tile([P, BLOCKS], F32, name="bias")
        nc.sync.dma_start(bias[:], b.rearrange("(p c) o -> p (c o)", c=BLOCKS))
        turns = []
        for d, lst in enumerate((pos1, pos2)):
            turn = keep.tile([P, V // 16], U16, name=f"turn{d}")
            nc.sync.dma_start(turn[:], lst)
            turns.append(turn)
        gates = tile([P, D, BLOCKS * V], F32, "gates")
        for d in range(D):
            nc.sync.dma_start(gates[:, d, :], gate[d].rearrange("(p c) v -> p (c v)", c=BLOCKS))

        got01 = tile([P, 2, S], F32, "got01")
        got23 = tile([P, 2, SLICE], F32, "got23")
        grouped = tile([P, S, PACK], BF16, "grouped")
        x_codes = tile([P, S], U32, "x_codes")
        x_scales = tile([P, S], U8, "x_scales")
        w_grouped = [tile([P, P, PACK], BF16, f"w_grouped{c}") for c in range(BLOCKS)]
        w_codes = [tile([P, P], U32, f"w_codes{c}") for c in range(BLOCKS)]
        w_scales = [tile([P, P], U8, f"w_scales{c}") for c in range(BLOCKS)]
        y = [tile([P, S], F32, f"y{c}") for c in range(BLOCKS)]
        w_by_block = w_raw[:].rearrange("p j (m c) -> p c m j", c=BLOCKS)

        def cut(s):
            return slice(s * SLICE, (s + 1) * SLICE)

        def fetch_a(j):
            nc.vector.tensor_copy(got23[:, j - 2, :], planes[j][:].indirect(nodes[:, 0 : SLICE // 16]))

        def fetch_b(j):
            nc.vector.tensor_copy(grouped[:, SLICE:S, j], planes[j][:].indirect(nodes[:, SLICE // 16 : S // 16]))

        def pair01():
            nc.scalar.copy(grouped[:, :, 0:2], got01[:].rearrange("p j s -> p s j"))

        def pair23():
            nc.scalar.copy(grouped[:, cut(0), 2:4], got23[:].rearrange("p j s -> p s j"))

        def quantize(codes, scales, values):
            nc.vector.quantize_mx(out=codes.bitcast(FP8X4), scales=scales, in_=values)

        def quantize_x(s):
            quantize(x_codes[:, cut(s)], x_scales[:, cut(s)], grouped[:, cut(s), :].rearrange("p s j -> p (s j)"))

        def quantize_w(c):
            quantize(w_codes[c][:], w_scales[c][:], w_grouped[c][:].rearrange("p m j -> p (m j)"))

        def multiply(c, s, on_vector=False):
            acc = psum.tile([P, SLICE], F32, name=f"acc{c}{s}")
            nc.tensor.matmul_mx(
                out=acc[:],
                lhsT=w_codes[c][:].bitcast(FP8X4),
                lhsT_scale=w_scales[c][:],
                rhs=x_codes[:, cut(s)].bitcast(FP8X4),
                rhs_scale=x_scales[:, cut(s)],
                start=True,
                stop=True,
            )
            if on_vector:
                nc.vector.tensor_scalar(y[c][:, cut(s)], acc[:], bias[:, c : c + 1], 0.0, ADD, MAX)
            else:
                nc.scalar.activation(y[c][:, cut(s)], acc[:], RELU, bias=bias[:, c : c + 1])

        prods = {}

        def fetch(c, d):
            prods[c, d] = tile([P, V], F32, f"prod{c}{d}")
            nc.vector.tensor_tensor(
                prods[c, d][:], y[c][:].indirect(turns[d][:]), gates[:, d, c * V : (c + 1) * V], MULT
            )

        def finish(c):
            total = tile([P, V], F32, f"total{c}")
            nc.vector.tensor_tensor(total[:], prods[c, 0][:], prods[c, 1][:], ADD)
            nc.sync.dma_start(out.rearrange("(p c) v -> p c v", c=BLOCKS)[:, c, :], total[:])

        for j in (0, 1):
            nc.vector.tensor_copy(got01[:, j, :], planes[j][:].indirect(nodes[:]))
        pair01()
        fetch_a(2)
        fetch_b(2)
        fetch_a(3)
        pair23()
        nc.scalar.copy(w_grouped[0][:], w_by_block[:, 0])
        fetch_b(3)
        quantize_x(0)
        quantize_w(0)
        multiply(0, 0)
        quantize_x(1)
        multiply(0, 1)
        quantize_x(2)
        multiply(0, 2)
        nc.scalar.copy(w_grouped[1][:], w_by_block[:, 1])
        quantize_w(1)
        multiply(1, 0)
        multiply(1, 1)
        multiply(1, 2)

        fetch(0, 0)
        fetch(0, 1)
        fetch(1, 0)
        fetch(1, 1)
        finish(0)
        finish(1)
